import numpy as np
import ml_dtypes


def mxq(x, axis, fmt="e4m3"):
    dtype, down = {"e4m3": (ml_dtypes.float8_e4m3fn, 7), "e5m2": (ml_dtypes.float8_e5m2, 14)}[fmt]
    v = np.moveaxis(np.asarray(x, np.float32).astype(ml_dtypes.bfloat16).astype(np.float64), axis, -1)
    blocks = v.reshape(v.shape[:-1] + (-1, 32))
    amax = np.abs(blocks).max(-1, keepdims=True)
    byte = np.maximum(np.where(amax > 0, np.frexp(amax)[1] - 1 + 127, 0) - down, 1)
    scale = np.exp2(byte - 127.0)
    codes = (blocks / scale).astype(np.float32).astype(dtype).astype(np.float64)
    return np.moveaxis((codes * scale).reshape(v.shape), -1, axis)


WIDE = False


def mx_kscale(k):
    if not WIDE:
        return np.ones(k)
    levels = np.array([30, -30])
    if k % 512:
        return np.exp2(np.random.permutation(np.resize(levels, k // 32))).repeat(32)
    a = np.empty((k // 512, 16))
    for p in range(k // 512):
        a[p, :8] = np.random.permutation(np.resize(levels, 8))
        for g in range(8):
            far = levels[np.abs(levels - a[p, g]) >= 10]
            a[p, g + 8] = far[np.random.randint(len(far))]
    return np.exp2(a.ravel()).repeat(32)


def f64(x):
    return np.asarray(x).astype(np.float64)


def striped(idx):
    return np.tile(np.asarray(idx).reshape(-1, 16).T, (8, 1)).astype(np.uint16)


def unstriped(offs):
    return offs[:16].T.reshape(-1).astype(np.int64)


def striped8(idx):
    return np.asarray(idx).reshape(8, -1, 16).transpose(0, 2, 1).reshape(128, -1).astype(np.uint16)


def unstriped8(offs):
    return offs.reshape(8, 16, -1).transpose(0, 2, 1).reshape(8, -1).astype(np.int64)


def pick8(x, idx, run):
    r = np.arange(len(x))
    return x[r[:, None], idx[r % (8 * run) // run]]


E2M1 = np.array([0.0, 0.5, 1.0, 1.5, 2.0, 3.0, 4.0, 6.0, -0.0, -0.5, -1.0, -1.5, -2.0, -3.0, -4.0, -6.0])


def pack_weight(w, fmt):
    k, n = w.shape
    w = f64(np.asarray(w, np.float32).astype(ml_dtypes.bfloat16)).reshape(k // 32, 32, n)
    amax = np.abs(w).max(1)
    if fmt in ("e4m3", "e5m2"):
        byte = np.frexp(amax)[1] - 1 + 127 - (7 if fmt == "e4m3" else 14)
    else:
        mant, ex = np.frexp(amax / 6.0)
        byte = np.where(mant > 0.5, ex, ex - 1) + 127
    byte = np.clip(np.where(amax > 0, byte, 1), 1, 254)
    scaled = (w * np.exp2(127.0 - byte)[:, None, :]).reshape(k, n).astype(np.float32)
    by_word = np.ascontiguousarray(scaled.reshape(k // 512, 128, 4, n).transpose(0, 1, 3, 2))
    if fmt in ("e4m3", "e5m2"):
        words = by_word.astype(ml_dtypes.float8_e4m3fn if fmt == "e4m3" else ml_dtypes.float8_e5m2).view(np.uint8)
    else:
        c = by_word.astype(ml_dtypes.float4_e2m1fn).view(np.uint8) & 0xF
        words = (c[..., 0::2] | (c[..., 1::2] << 4)).reshape(k // 512, 128, 2 * n)
    return np.ascontiguousarray(words), np.ascontiguousarray(byte.astype(np.uint8).reshape(k // 512, 16, n))


def unpack_weight(words, scales, fmt):
    g, _, n = scales.shape
    words = np.ascontiguousarray(words).reshape(g, 128, n, -1)
    if fmt in ("e4m3", "e5m2"):
        vals = words.view(ml_dtypes.float8_e4m3fn if fmt == "e4m3" else ml_dtypes.float8_e5m2).astype(np.float64)
    else:
        nib = np.empty((g, 128, n, 4), np.uint8)
        nib[..., 0::2] = words & 0xF
        nib[..., 1::2] = words >> 4
        vals = E2M1[nib]
    vals = vals * np.repeat(np.exp2(scales.astype(np.float64) - 127.0), 8, axis=1)[..., None]
    return vals.transpose(0, 1, 3, 2).reshape(g * 512, n)


K, T, J, R, F, Z, C, N = 512, 1024, 256, 512, 512, 1024, 512, 256


def setup_inputs():
    n = np.random.standard_normal
    idx = np.random.permutation(T)[:J]
    idx2 = np.random.permutation(Z)[:J]
    idx3 = np.stack([np.random.permutation(C)[:J] for _ in range(8)])
    idx4 = np.stack([np.random.permutation(C)[:J] for _ in range(8)])
    fk = mx_kscale(K)
    ff = mx_kscale(F)
    fr = mx_kscale(R)
    xtp = pack_weight(n((K, T)) / fk[:, None], "e2m1")
    xop = pack_weight(n((F, Z)) / ff[:, None], "e5m2")
    wp = pack_weight(n((K, R)) * 1 / np.sqrt(K) * fk[:, None] * fr, "e5m2")
    w0p = pack_weight(n((F, R)) * 1 / np.sqrt(F) * ff[:, None] * fr, "e4m3")
    w2p = pack_weight(n((F, R)) * 1 / np.sqrt(F) * ff[:, None] * fr, "e4m3")
    wbp = pack_weight(n((R, N)) * 1 / np.sqrt(R) / fr[:, None], "e4m3")
    return {
        "xt_words": xtp[0],
        "xt_scales": xtp[1],
        "xo_words": xop[0],
        "xo_scales": xop[1],
        "w_words": wp[0],
        "w_scales": wp[1],
        "w0_words": w0p[0],
        "w0_scales": w0p[1],
        "w2_words": w2p[0],
        "w2_scales": w2p[1],
        "wb_words": wbp[0],
        "wb_scales": wbp[1],
        "offs": striped(idx),
        "offs2": striped(idx2),
        "offs3": striped8(idx3),
        "offs4": striped8(idx4),
    }


def reference(xt_words, xt_scales, xo_words, xo_scales, w_words, w_scales, w0_words, w0_scales, w2_words, w2_scales, wb_words, wb_scales, offs, offs2, offs3, offs4):
    idx = unstriped(offs)
    idx2 = unstriped(offs2)
    idx3 = unstriped8(offs3)
    idx4 = unstriped8(offs4)
    xtu = unpack_weight(xt_words, xt_scales, "e2m1")
    xou = unpack_weight(xo_words, xo_scales, "e5m2")
    wu = unpack_weight(w_words, w_scales, "e5m2")
    w0u = unpack_weight(w0_words, w0_scales, "e4m3")
    w2u = unpack_weight(w2_words, w2_scales, "e4m3")
    wbu = unpack_weight(wb_words, wb_scales, "e4m3")
    xtidxg = xtu[:, idx]
    xoidx2g = xou[:, idx2]
    a = wu.T @ xtidxg + w0u.T @ xoidx2g
    b = w2u.T @ xoidx2g
    pa = np.zeros((R, C))
    pa[np.arange(R)[:, None], idx3[np.arange(R) % 512 // 64]] = a
    pb = np.zeros((R, C))
    pb[np.arange(R)[:, None], idx4[np.arange(R) % 512 // 64]] = b
    pl = np.pad(pb, ((0, 0), (1, 0)))[:, :C]
    hid = np.abs(pa - pl)
    hidq = mxq(hid, 0, "e4m3")
    p = wbu.T @ hidq
    return p

@@ -1,0 +1,205 @@
+from contextlib import ExitStack
+
+import concourse.mybir as mybir
+
+K, T, J, R, F, Z, C, N = 512, 1024, 256, 512, 512, 1024, 512, 256
+FLOPS = 2 * K * R * J + 2 * 2 * F * R * J + 2 * R * N * C
+
+F32 = mybir.dt.float32
+BF16 = mybir.dt.bfloat16
+I32 = mybir.dt.int32
+U32 = mybir.dt.uint32
+U16 = mybir.dt.uint16
+U8 = mybir.dt.uint8
+E4M3 = mybir.dt.float8_e4m3fn_x4
+E5M2 = mybir.dt.float8_e5m2_x4
+E2M1 = mybir.dt.float4_e2m1fn_x4
+ACT = mybir.ActivationFunctionType
+ALU = mybir.AluOpType
+
+P = 128
+PACK = 4
+QUADS = 4
+CHUNK = 128
+CHUNKS = C // CHUNK
+
+
+def tile_list_laggedboards_kernel(tc, xt_words, xt_scales, xo_words, xo_scales, w_words, w_scales,
+                                        w0_words, w0_scales, w2_words, w2_scales, wb_words, wb_scales,
+                                        offs, offs2, offs3, offs4, out):
+    nc = tc.nc
+    with ExitStack() as ctx:
+        sb = ctx.enter_context(tc.tile_pool(name="sb", bufs=1))
+        ps = ctx.enter_context(tc.psum_pool(name="ps", bufs=1))
+
+        def tile(name, shape, dtype, tag=None):
+            return sb.tile(shape, dtype, name=name, tag=tag or name, align_bytes=64)
+
+        def load_list(name, src):
+            lst = sb.tile([P, J // 16], U16, name=name)
+            nc.sync.dma_start(lst[:], src)
+            return lst
+
+        def load_words(name, src):
+            words = tile(name, [P, src.shape[2]], I32)
+            nc.sync.dma_start(words[:], src[0].rearrange("p n t -> p (n t)").bitcast(I32))
+            return words
+
+        def zeroed_plane(name, width):
+            plane = tile(name, [P, width], U8)
+            nc.vector.memset(plane[:].bitcast(I32), 0)
+            return plane
+
+        def load_plane(plane, src):
+            for q in range(QUADS):
+                nc.sync.dma_start(plane[32 * q:32 * q + 4, :].bitcast(I32), src[0, 4 * q:4 * q + 4, :].bitcast(I32))
+
+        def stage_rows(stage, slot, src):
+            nc.sync.dma_start(stage[:, :, slot, :], src[0].bitcast(I32).rearrange("(q r) n -> r q n", r=4))
+
+        def spread_rows(plane, stage):
+            for q in range(QUADS):
+                nc.vector.tensor_copy(plane[32 * q:32 * q + 4, :].bitcast(I32),
+                                      stage[:, q, :, :].rearrange("r s n -> r (s n)"))
+
+        def deal(name, raw, dtype, count):
+            dealt = tile(name, [P, count, PACK, P], dtype)
+            nc.vector.tensor_copy(dealt[:].rearrange("p s t m -> p s m t"),
+                                  raw[:].rearrange("p (s m t) -> p s m t", s=count, t=PACK))
+            return dealt
+
+        def gather(picked, window, lst, lo, hi):
+            nc.vector.tensor_copy(picked[:], window.indirect(lst[:, lo // 16:hi // 16]))
+
+        def board(name, tag=None):
+            page = tile(name, [P, C], F32, tag)
+            nc.vector.memset(page[:].bitcast(I32), 0)
+            return page
+
+        list2 = load_list("list2", offs2)
+        xo_stage = tile("xo_stage", [4, QUADS, 1, Z // 4], I32)
+        stage_rows(xo_stage, 0, xo_scales)
+        w2_stage = tile("w2_stage", [4, QUADS, 1, R // 4], I32)
+        stage_rows(w2_stage, 0, w2_scales)
+        xo_all = load_words("xo_all", xo_words)
+        w2_raw = load_words("w2_raw", w2_words)
+        list4 = load_list("list4", offs4)
+
+        xo_plane = zeroed_plane("xo_plane", Z)
+        w2_plane = zeroed_plane("w2_plane", R)
+        pb = [board("pb0"), board("pb1")]
+
+        list1 = load_list("list1", offs)
+        xt_all = tile("xt_all", [P, T], U16)
+        nc.sync.dma_start(xt_all[:].bitcast(I32), xt_words[0].bitcast(I32))
+        w_raw = load_words("w_raw", w_words)
+        w0_raw = load_words("w0_raw", w0_words)
+        list3 = load_list("list3", offs3)
+        wb_codes = load_words("wb_codes", wb_words)
+        xt_plane = zeroed_plane("xt_plane", T)
+        load_plane(xt_plane[:], xt_scales)
+        ww0_plane = zeroed_plane("ww0_plane", 2 * R)
+        load_plane(ww0_plane[:, 0:R], w_scales)
+        load_plane(ww0_plane[:, R:2 * R], w0_scales)
+        wb_plane = zeroed_plane("wb_plane", N)
+        load_plane(wb_plane[:], wb_scales)
+
+        half = J // 2
+        xo_window = xo_all[:].bitcast(U32)
+        spread_rows(xo_plane, xo_stage)
+        spread_rows(w2_plane, w2_stage)
+        xo_sc = [tile("xo_sc0", [P, half], U8)]
+        xo_codes = [tile("xo_codes0", [P, half], U32)]
+        gather(xo_sc[0], xo_plane[:], list2, 0, half)
+        w2_sc = deal("w2_sc", w2_plane, U8, 1)
+        gather(xo_codes[0], xo_window, list2, 0, half)
+        w2_codes = deal("w2_codes", w2_raw, I32, 1)
+
+        def b_piece(t, halves, bank):
+            acc = ps.tile([P, len(halves), half], F32, name="acc_b%d_%d" % (t, halves[0]), tag="bank%d" % bank)
+            for i, u in enumerate(halves):
+                nc.tensor.matmul_mx(out=acc[:, i, :], lhsT=w2_codes[:, 0, t, :].bitcast(E4M3), lhsT_scale=w2_sc[:, 0, t, :],
+                                    rhs=xo_codes[u][:].bitcast(E5M2), rhs_scale=xo_sc[u][:], start=True, stop=True)
+            vals = tile("b%d_%d" % (t, halves[0]), [P, len(halves) * half], F32)
+            flat = acc[:].rearrange("p u j -> p (u j)")
+            if bank == 0:
+                nc.scalar.activation(vals[:], flat, ACT.Copy)
+            else:
+                nc.vector.tensor_copy(vals[:], flat)
+            lo, hi = halves[0] * half, (halves[-1] + 1) * half
+            nc.scalar.activation(pb[t][:].indirect(list4[:, lo // 16:hi // 16]), vals[:], ACT.Copy)
+
+        b_piece(0, (0,), 0)
+        xo_sc.append(tile("xo_sc1", [P, half], U8, "w2_plane"))
+        xo_codes.append(tile("xo_codes1", [P, half], U32, "w2_raw"))
+        gather(xo_sc[1], xo_plane[:], list2, half, J)
+        gather(xo_codes[1], xo_window, list2, half, J)
+        b_piece(0, (1,), 1)
+        for t in range(1, PACK):
+            if t > 1:
+                pb.append(board("pb%d" % t, ("xo_all", "xo_plane")[t - 2]))
+            b_piece(t, (0, 1), 1 + t)
+
+        xt_sc = tile("xt_sc", [P, J], U8)
+        xt_codes = tile("xt_codes", [P, J], U16)
+        gather(xt_codes, xt_all[:], list1, 0, J)
+        w_codes = deal("w_codes", w_raw, I32, 1)
+        w0_codes = deal("w0_codes", w0_raw, I32, 1)
+        gather(xt_sc, xt_plane[:], list1, 0, J)
+        ww0_sc = deal("ww0_sc", ww0_plane, U8, 2)
+
+        pa = []
+        for t in range(PACK):
+            acc = ps.tile([P, J], F32, name="acc_a%d" % t, tag="bank%d" % ((5 + t) % 8))
+            nc.tensor.matmul_mx(out=acc[:], lhsT=w_codes[:, 0, t, :].bitcast(E5M2), lhsT_scale=ww0_sc[:, 0, t, :],
+                                rhs=xt_codes[:].bitcast(E2M1), rhs_scale=xt_sc[:], start=True, stop=False)
+            for u in range(2):
+                nc.tensor.matmul_mx(out=acc[:, u * half:(u + 1) * half], lhsT=w0_codes[:, 0, t, :].bitcast(E4M3),
+                                    lhsT_scale=ww0_sc[:, 1, t, :], rhs=xo_codes[u][:].bitcast(E5M2),
+                                    rhs_scale=xo_sc[u][:], start=False, stop=(u == 1))
+            vals = tile("a%d" % t, [P, J], F32)
+            nc.vector.tensor_copy(vals[:], acc[:])
+            page = board("pa%d" % t, ("xt_all", "w_raw", "w0_raw", "ww0_plane")[t])
+            nc.scalar.activation(page[:].indirect(list3[:]), vals[:], ACT.Copy)
+            pa.append(page)
+
+        def difference(dst, t, lo, hi):
+            first = max(lo, 1)
+            nc.vector.tensor_tensor(dst[:, first - lo:hi - lo], pa[t][:, first:hi], pb[t][:, first - 1:hi - 1],
+                                    ALU.subtract)
+            if lo == 0:
+                nc.vector.tensor_copy(dst[:, 0:1], pa[t][:, 0:1])
+
+        d01 = tile("d01", [P, 2, C], F32)
+        for t in range(2):
+            difference(d01[:, t, :], t, 0, C)
+        hid = [tile("hid%d" % k, [P, CHUNK, PACK], BF16) for k in range(CHUNKS)]
+        for k in range(CHUNKS):
+            pair = d01[:, :, k * CHUNK:(k + 1) * CHUNK].rearrange("p t c -> p c t")
+            nc.vector.scalar_tensor_tensor(hid[k][:, :, 0:2], pair, -1.0, pair, ALU.mult, ALU.max)
+        d23 = [tile("d23_%d" % k, [P, 2, CHUNK], F32) for k in range(CHUNKS)]
+        order = list(reversed(range(CHUNKS)))
+        for t in range(2, PACK):
+            for k in order:
+                difference(d23[k][:, t - 2, :], t, k * CHUNK, (k + 1) * CHUNK)
+        out_v = out.rearrange("(h p) c -> p h c", p=P)
+        for k in order:
+            nc.scalar.activation(hid[k][:, :, 2:4], d23[k][:].rearrange("p t c -> p c t"), ACT.Abs)
+        sums = []
+        for k in order:
+            hq = tile("hq%d" % k, [P, CHUNK], U32)
+            hs = tile("hs%d" % k, [P, CHUNK], U8)
+            nc.vector.quantize_mx(out=hq[:].bitcast(E4M3), scales=hs[:], in_=hid[k][:].rearrange("p c t -> p (c t)"))
+            acc = ps.tile([P, N // P, CHUNK], F32, name="acc_o%d" % k, tag="bank%d" % (1 + k))
+            for h in range(N // P):
+                cols = slice(h * P, (h + 1) * P)
+                nc.tensor.matmul_mx(out=acc[:, h, :], lhsT=wb_codes[:, cols].bitcast(E4M3), lhsT_scale=wb_plane[:, cols],
+                                    rhs=hq[:].bitcast(E4M3), rhs_scale=hs[:], start=True, stop=True)
+            sums.append(acc)
+        for k, acc in zip(order, sums):
+            res = tile("res%d" % k, [P, N // P, CHUNK], F32)
+            if k % 2 == 0:
+                nc.vector.tensor_copy(res[:], acc[:])
+            else:
+                nc.scalar.copy(res[:], acc[:])
+            nc.sync.dma_start(out_v[:, :, k * CHUNK:(k + 1) * CHUNK], res[:])

@@ -40,14 +40,14 @@ def tile_list_laggedboards_kernel(tc, xt_words, xt_scales, xo_words, xo_scales, 
             nc.sync.dma_start(lst[:], src)
             return lst
 
-        def load_words(name, src):
-            words = tile(name, [P, src.shape[2]], I32)
+        def load_words(name, src, tag=None):
+            words = tile(name, [P, src.shape[2]], I32, tag)
             nc.sync.dma_start(words[:], src[0].rearrange("p n t -> p (n t)").bitcast(I32))
             return words
 
-        def zeroed_plane(name, width):
+        def zeroed_plane(name, width, engine):
             plane = tile(name, [P, width], U8)
-            nc.vector.memset(plane[:].bitcast(I32), 0)
+            engine.memset(plane[:].bitcast(I32), 0)
             return plane
 
         def load_plane(plane, src):
@@ -62,18 +62,18 @@ def tile_list_laggedboards_kernel(tc, xt_words, xt_scales, xo_words, xo_scales, 
                 nc.vector.tensor_copy(plane[32 * q:32 * q + 4, :].bitcast(I32),
                                       stage[:, q, :, :].rearrange("r s n -> r (s n)"))
 
-        def deal(name, raw, dtype, count):
-            dealt = tile(name, [P, count, PACK, P], dtype)
-            nc.vector.tensor_copy(dealt[:].rearrange("p s t m -> p s m t"),
-                                  raw[:].rearrange("p (s m t) -> p s m t", s=count, t=PACK))
-            return dealt
+        def deal(name, raw, dtype, copy, t0=0, t1=PACK):
+            dealt = tile(name, [P, t1 - t0, P], dtype)
+            copy(dealt[:].rearrange("p t m -> p m t"),
+                 raw[:].bitcast(dtype).rearrange("p (m t) -> p m t", t=PACK)[:, :, t0:t1])
+            return [dealt[:, t, :] for t in range(t1 - t0)]
 
         def gather(picked, window, lst, lo, hi):
             nc.vector.tensor_copy(picked[:], window.indirect(lst[:, lo // 16:hi // 16]))
 
-        def board(name, tag=None):
+        def board(name, engine, tag=None):
             page = tile(name, [P, C], F32, tag)
-            nc.vector.memset(page[:].bitcast(I32), 0)
+            engine.memset(page[:].bitcast(I32), 0)
             return page
 
         list2 = load_list("list2", offs2)
@@ -85,9 +85,9 @@ def tile_list_laggedboards_kernel(tc, xt_words, xt_scales, xo_words, xo_scales, 
         w2_raw = load_words("w2_raw", w2_words)
         list4 = load_list("list4", offs4)
 
-        xo_plane = zeroed_plane("xo_plane", Z)
-        w2_plane = zeroed_plane("w2_plane", R)
-        pb = [board("pb0"), board("pb1")]
+        xo_plane = zeroed_plane("xo_plane", Z, nc.vector)
+        w2_plane = zeroed_plane("w2_plane", R, nc.vector)
+        pb = [board("pb0", nc.vector)]
 
         list1 = load_list("list1", offs)
         xt_all = tile("xt_all", [P, T], U16)
@@ -95,30 +95,32 @@ def tile_list_laggedboards_kernel(tc, xt_words, xt_scales, xo_words, xo_scales, 
         w_raw = load_words("w_raw", w_words)
         w0_raw = load_words("w0_raw", w0_words)
         list3 = load_list("list3", offs3)
-        wb_codes = load_words("wb_codes", wb_words)
-        xt_plane = zeroed_plane("xt_plane", T)
+        xt_plane = zeroed_plane("xt_plane", T, nc.gpsimd)
         load_plane(xt_plane[:], xt_scales)
-        ww0_plane = zeroed_plane("ww0_plane", 2 * R)
-        load_plane(ww0_plane[:, 0:R], w_scales)
-        load_plane(ww0_plane[:, R:2 * R], w0_scales)
-        wb_plane = zeroed_plane("wb_plane", N)
-        load_plane(wb_plane[:], wb_scales)
+        w_plane = zeroed_plane("w_plane", R, nc.gpsimd)
+        load_plane(w_plane[:], w_scales)
+        w0_plane = zeroed_plane("w0_plane", R, nc.gpsimd)
+        load_plane(w0_plane[:], w0_scales)
+        wb_plane = zeroed_plane("wb_plane", N, nc.gpsimd)
+        pb.append(board("pb1", nc.gpsimd))
 
         half = J // 2
         xo_window = xo_all[:].bitcast(U32)
         spread_rows(xo_plane, xo_stage)
         spread_rows(w2_plane, w2_stage)
+        wb_codes = load_words("wb_codes", wb_words, "xo_stage")
+        load_plane(wb_plane[:], wb_scales)
         xo_sc = [tile("xo_sc0", [P, half], U8)]
         xo_codes = [tile("xo_codes0", [P, half], U32)]
         gather(xo_sc[0], xo_plane[:], list2, 0, half)
-        w2_sc = deal("w2_sc", w2_plane, U8, 1)
+        w2_sc = deal("w2_sc_first", w2_plane, U8, nc.vector.tensor_copy, 0, 1)
         gather(xo_codes[0], xo_window, list2, 0, half)
-        w2_codes = deal("w2_codes", w2_raw, I32, 1)
+        w2_codes = deal("w2_codes_first", w2_raw, I32, nc.vector.tensor_copy, 0, 1)
 
         def b_piece(t, halves, bank):
             acc = ps.tile([P, len(halves), half], F32, name="acc_b%d_%d" % (t, halves[0]), tag="bank%d" % bank)
             for i, u in enumerate(halves):
-                nc.tensor.matmul_mx(out=acc[:, i, :], lhsT=w2_codes[:, 0, t, :].bitcast(E4M3), lhsT_scale=w2_sc[:, 0, t, :],
+                nc.tensor.matmul_mx(out=acc[:, i, :], lhsT=w2_codes[t].bitcast(E4M3), lhsT_scale=w2_sc[t],
                                     rhs=xo_codes[u][:].bitcast(E5M2), rhs_scale=xo_sc[u][:], start=True, stop=True)
             vals = tile("b%d_%d" % (t, halves[0]), [P, len(halves) * half], F32)
             flat = acc[:].rearrange("p u j -> p (u j)")
@@ -130,36 +132,39 @@ def tile_list_laggedboards_kernel(tc, xt_words, xt_scales, xo_words, xo_scales, 
             nc.scalar.activation(pb[t][:].indirect(list4[:, lo // 16:hi // 16]), vals[:], ACT.Copy)
 
         b_piece(0, (0,), 0)
-        xo_sc.append(tile("xo_sc1", [P, half], U8, "w2_plane"))
-        xo_codes.append(tile("xo_codes1", [P, half], U32, "w2_raw"))
+        xo_sc.append(tile("xo_sc1", [P, half], U8))
+        xo_codes.append(tile("xo_codes1", [P, half], U32))
         gather(xo_sc[1], xo_plane[:], list2, half, J)
         gather(xo_codes[1], xo_window, list2, half, J)
+        w2_sc.extend(deal("w2_sc_rest", w2_plane, U8, nc.vector.tensor_copy, 1, PACK))
+        w2_codes.extend(deal("w2_codes_rest", w2_raw, I32, nc.vector.tensor_copy, 1, PACK))
         b_piece(0, (1,), 1)
         for t in range(1, PACK):
             if t > 1:
-                pb.append(board("pb%d" % t, ("xo_all", "xo_plane")[t - 2]))
+                pb.append(board("pb%d" % t, nc.gpsimd, ("xo_all", "xo_plane")[t - 2]))
             b_piece(t, (0, 1), 1 + t)
 
         xt_sc = tile("xt_sc", [P, J], U8)
         xt_codes = tile("xt_codes", [P, J], U16)
         gather(xt_codes, xt_all[:], list1, 0, J)
-        w_codes = deal("w_codes", w_raw, I32, 1)
-        w0_codes = deal("w0_codes", w0_raw, I32, 1)
+        w_codes = deal("w_codes", w_raw, I32, nc.vector.tensor_copy)
+        w0_codes = deal("w0_codes", w0_raw, I32, nc.vector.tensor_copy)
         gather(xt_sc, xt_plane[:], list1, 0, J)
-        ww0_sc = deal("ww0_sc", ww0_plane, U8, 2)
+        w_sc = deal("w_sc", w_plane, U8, nc.vector.tensor_copy)
+        w0_sc = deal("w0_sc", w0_plane, U8, nc.vector.tensor_copy)
 
         pa = []
         for t in range(PACK):
             acc = ps.tile([P, J], F32, name="acc_a%d" % t, tag="bank%d" % ((5 + t) % 8))
-            nc.tensor.matmul_mx(out=acc[:], lhsT=w_codes[:, 0, t, :].bitcast(E5M2), lhsT_scale=ww0_sc[:, 0, t, :],
+            nc.tensor.matmul_mx(out=acc[:], lhsT=w_codes[t].bitcast(E5M2), lhsT_scale=w_sc[t],
                                 rhs=xt_codes[:].bitcast(E2M1), rhs_scale=xt_sc[:], start=True, stop=False)
             for u in range(2):
-                nc.tensor.matmul_mx(out=acc[:, u * half:(u + 1) * half], lhsT=w0_codes[:, 0, t, :].bitcast(E4M3),
-                                    lhsT_scale=ww0_sc[:, 1, t, :], rhs=xo_codes[u][:].bitcast(E5M2),
+                nc.tensor.matmul_mx(out=acc[:, u * half:(u + 1) * half], lhsT=w0_codes[t].bitcast(E4M3),
+                                    lhsT_scale=w0_sc[t], rhs=xo_codes[u][:].bitcast(E5M2),
                                     rhs_scale=xo_sc[u][:], start=False, stop=(u == 1))
             vals = tile("a%d" % t, [P, J], F32)
             nc.vector.tensor_copy(vals[:], acc[:])
-            page = board("pa%d" % t, ("xt_all", "w_raw", "w0_raw", "ww0_plane")[t])
+            page = board("pa%d" % t, nc.gpsimd, ("xt_all", "w_raw", "w0_raw", "xt_plane")[t])
             nc.scalar.activation(page[:].indirect(list3[:]), vals[:], ACT.Copy)
             pa.append(page)
 
@@ -178,13 +183,16 @@ def tile_list_laggedboards_kernel(tc, xt_words, xt_scales, xo_words, xo_scales, 
             pair = d01[:, :, k * CHUNK:(k + 1) * CHUNK].rearrange("p t c -> p c t")
             nc.vector.scalar_tensor_tensor(hid[k][:, :, 0:2], pair, -1.0, pair, ALU.mult, ALU.max)
         d23 = [tile("d23_%d" % k, [P, 2, CHUNK], F32) for k in range(CHUNKS)]
-        order = list(reversed(range(CHUNKS)))
-        for t in range(2, PACK):
-            for k in order:
-                difference(d23[k][:, t - 2, :], t, k * CHUNK, (k + 1) * CHUNK)
+        for k in range(CHUNKS):
+            difference(d23[k][:, 0, :], 2, k * CHUNK, (k + 1) * CHUNK)
+        for k in (3, 2, 1, 0):
+            difference(d23[k][:, 1, :], 3, k * CHUNK, (k + 1) * CHUNK)
         out_v = out.rearrange("(h p) c -> p h c", p=P)
-        for k in order:
+        for k in (3, 2, 1):
             nc.scalar.activation(hid[k][:, :, 2:4], d23[k][:].rearrange("p t c -> p c t"), ACT.Abs)
+        pair = d23[0][:].rearrange("p t c -> p c t")
+        nc.vector.scalar_tensor_tensor(hid[0][:, :, 2:4], pair, -1.0, pair, ALU.mult, ALU.max)
+        order = (3, 2, 0, 1)
         sums = []
         for k in order:
             hq = tile("hq%d" % k, [P, CHUNK], U32)
@@ -198,7 +206,7 @@ def tile_list_laggedboards_kernel(tc, xt_words, xt_scales, xo_words, xo_scales, 
             sums.append(acc)
         for k, acc in zip(order, sums):
             res = tile("res%d" % k, [P, N // P, CHUNK], F32)
-            if k % 2 == 0:
+            if k == 0:
                 nc.vector.tensor_copy(res[:], acc[:])
             else:
                 nc.scalar.copy(res[:], acc[:])

@@ -62,10 +62,10 @@ def tile_list_laggedboards_kernel(tc, xt_words, xt_scales, xo_words, xo_scales, 
                 nc.vector.tensor_copy(plane[32 * q:32 * q + 4, :].bitcast(I32),
                                       stage[:, q, :, :].rearrange("r s n -> r (s n)"))
 
-        def deal(name, raw, dtype, copy, t0=0, t1=PACK):
+        def deal(name, raw, dtype, run, t0=0, t1=PACK):
             dealt = tile(name, [P, t1 - t0, P], dtype)
-            copy(dealt[:].rearrange("p t m -> p m t"),
-                 raw[:].bitcast(dtype).rearrange("p (m t) -> p m t", t=PACK)[:, :, t0:t1])
+            src = raw[:].rearrange("p (b i t) -> p b t i", i=run, t=PACK)[:, :, t0:t1, :]
+            nc.vector.tensor_copy(dealt[:].rearrange("p t (b i) -> p b t i", i=run), src)
             return [dealt[:, t, :] for t in range(t1 - t0)]
 
         def gather(picked, window, lst, lo, hi):
@@ -76,24 +76,19 @@ def tile_list_laggedboards_kernel(tc, xt_words, xt_scales, xo_words, xo_scales, 
             engine.memset(page[:].bitcast(I32), 0)
             return page
 
+        xo_plane = zeroed_plane("xo_plane", Z, nc.gpsimd)
         list2 = load_list("list2", offs2)
-        xo_stage = tile("xo_stage", [4, QUADS, 1, Z // 4], I32)
-        stage_rows(xo_stage, 0, xo_scales)
         w2_stage = tile("w2_stage", [4, QUADS, 1, R // 4], I32)
         stage_rows(w2_stage, 0, w2_scales)
+        load_plane(xo_plane[:], xo_scales)
         xo_all = load_words("xo_all", xo_words)
         w2_raw = load_words("w2_raw", w2_words)
         list4 = load_list("list4", offs4)
 
-        xo_plane = zeroed_plane("xo_plane", Z, nc.vector)
         w2_plane = zeroed_plane("w2_plane", R, nc.vector)
         pb = [board("pb0", nc.vector)]
 
         list1 = load_list("list1", offs)
-        xt_all = tile("xt_all", [P, T], U16)
-        nc.sync.dma_start(xt_all[:].bitcast(I32), xt_words[0].bitcast(I32))
-        w_raw = load_words("w_raw", w_words)
-        w0_raw = load_words("w0_raw", w0_words)
         list3 = load_list("list3", offs3)
         xt_plane = zeroed_plane("xt_plane", T, nc.gpsimd)
         load_plane(xt_plane[:], xt_scales)
@@ -106,16 +101,16 @@ def tile_list_laggedboards_kernel(tc, xt_words, xt_scales, xo_words, xo_scales, 
 
         half = J // 2
         xo_window = xo_all[:].bitcast(U32)
-        spread_rows(xo_plane, xo_stage)
         spread_rows(w2_plane, w2_stage)
-        wb_codes = load_words("wb_codes", wb_words, "xo_stage")
-        load_plane(wb_plane[:], wb_scales)
+        xt_all = tile("xt_all", [P, T], U16, "w2_stage")
+        nc.sync.dma_start(xt_all[:].bitcast(I32), xt_words[0].bitcast(I32))
         xo_sc = [tile("xo_sc0", [P, half], U8)]
         xo_codes = [tile("xo_codes0", [P, half], U32)]
         gather(xo_sc[0], xo_plane[:], list2, 0, half)
-        w2_sc = deal("w2_sc_first", w2_plane, U8, nc.vector.tensor_copy, 0, 1)
+        w2_sc = deal("w2_sc", w2_plane, U8, 16)
+        w_raw = load_words("w_raw", w_words, "w2_plane")
         gather(xo_codes[0], xo_window, list2, 0, half)
-        w2_codes = deal("w2_codes_first", w2_raw, I32, nc.vector.tensor_copy, 0, 1)
+        w2_codes = deal("w2_codes_first", w2_raw, I32, 4, 0, 1)
 
         def b_piece(t, halves, bank):
             acc = ps.tile([P, len(halves), half], F32, name="acc_b%d_%d" % (t, halves[0]), tag="bank%d" % bank)
@@ -136,8 +131,8 @@ def tile_list_laggedboards_kernel(tc, xt_words, xt_scales, xo_words, xo_scales, 
         xo_codes.append(tile("xo_codes1", [P, half], U32))
         gather(xo_sc[1], xo_plane[:], list2, half, J)
         gather(xo_codes[1], xo_window, list2, half, J)
-        w2_sc.extend(deal("w2_sc_rest", w2_plane, U8, nc.vector.tensor_copy, 1, PACK))
-        w2_codes.extend(deal("w2_codes_rest", w2_raw, I32, nc.vector.tensor_copy, 1, PACK))
+        w2_codes.extend(deal("w2_codes_rest", w2_raw, I32, 4, 1, PACK))
+        w0_raw = load_words("w0_raw", w0_words, "w2_raw")
         b_piece(0, (1,), 1)
         for t in range(1, PACK):
             if t > 1:
@@ -147,11 +142,14 @@ def tile_list_laggedboards_kernel(tc, xt_words, xt_scales, xo_words, xo_scales, 
         xt_sc = tile("xt_sc", [P, J], U8)
         xt_codes = tile("xt_codes", [P, J], U16)
         gather(xt_codes, xt_all[:], list1, 0, J)
-        w_codes = deal("w_codes", w_raw, I32, nc.vector.tensor_copy)
-        w0_codes = deal("w0_codes", w0_raw, I32, nc.vector.tensor_copy)
+        w_codes = deal("w_codes", w_raw, I32, 4)
+        w0_codes = deal("w0_codes", w0_raw, I32, 4)
         gather(xt_sc, xt_plane[:], list1, 0, J)
-        w_sc = deal("w_sc", w_plane, U8, nc.vector.tensor_copy)
-        w0_sc = deal("w0_sc", w0_plane, U8, nc.vector.tensor_copy)
+        w_sc = deal("w_sc", w_plane, U8, 16)
+        w0_sc = deal("w0_sc", w0_plane, U8, 16)
+
+        wb_codes = load_words("wb_codes", wb_words, "w_plane")
+        load_plane(wb_plane[:], wb_scales)
 
         pa = []
         for t in range(PACK):
@@ -164,7 +162,7 @@ def tile_list_laggedboards_kernel(tc, xt_words, xt_scales, xo_words, xo_scales, 
                                     rhs_scale=xo_sc[u][:], start=False, stop=(u == 1))
             vals = tile("a%d" % t, [P, J], F32)
             nc.vector.tensor_copy(vals[:], acc[:])
-            page = board("pa%d" % t, nc.gpsimd, ("xt_all", "w_raw", "w0_raw", "xt_plane")[t])
+            page = board("pa%d" % t, nc.gpsimd, ("w2_stage", "w2_plane", "xt_plane", "w2_raw")[t])
             nc.scalar.activation(page[:].indirect(list3[:]), vals[:], ACT.Copy)
             pa.append(page)
 
@@ -175,13 +173,14 @@ def tile_list_laggedboards_kernel(tc, xt_words, xt_scales, xo_words, xo_scales, 
             if lo == 0:
                 nc.vector.tensor_copy(dst[:, 0:1], pa[t][:, 0:1])
 
-        d01 = tile("d01", [P, 2, C], F32)
+        mag01 = tile("mag01", [P, 2, C], F32)
         for t in range(2):
-            difference(d01[:, t, :], t, 0, C)
+            diff = tile("diff%d" % t, [P, C], F32)
+            difference(diff, t, 0, C)
+            nc.vector.scalar_tensor_tensor(mag01[:, t, :], diff[:], -1.0, diff[:], ALU.mult, ALU.max)
         hid = [tile("hid%d" % k, [P, CHUNK, PACK], BF16) for k in range(CHUNKS)]
         for k in range(CHUNKS):
-            pair = d01[:, :, k * CHUNK:(k + 1) * CHUNK].rearrange("p t c -> p c t")
-            nc.vector.scalar_tensor_tensor(hid[k][:, :, 0:2], pair, -1.0, pair, ALU.mult, ALU.max)
+            nc.vector.tensor_copy(hid[k][:, :, 0:2], mag01[:, :, k * CHUNK:(k + 1) * CHUNK].rearrange("p t c -> p c t"))
         d23 = [tile("d23_%d" % k, [P, 2, CHUNK], F32) for k in range(CHUNKS)]
         for k in range(CHUNKS):
             difference(d23[k][:, 0, :], 2, k * CHUNK, (k + 1) * CHUNK)

@@ -76,13 +76,16 @@ def tile_list_laggedboards_kernel(tc, xt_words, xt_scales, xo_words, xo_scales, 
             engine.memset(page[:].bitcast(I32), 0)
             return page
 
-        xo_plane = zeroed_plane("xo_plane", Z, nc.gpsimd)
+        xo_plane = tile("xo_plane", [P, Z], U8)
         list2 = load_list("list2", offs2)
         w2_stage = tile("w2_stage", [4, QUADS, 1, R // 4], I32)
         stage_rows(w2_stage, 0, w2_scales)
-        load_plane(xo_plane[:], xo_scales)
-        xo_all = load_words("xo_all", xo_words)
+        for q in range(QUADS):
+            rows = xo_scales[0, 4 * q:4 * q + 4, :].bitcast(I32)
+            nc.sync.dma_start(xo_plane[32 * q:32 * q + 32, :].bitcast(I32),
+                              rows.unsqueeze(0).broadcast_to([8, 4, Z // 4]))
         w2_raw = load_words("w2_raw", w2_words)
+        xo_all = load_words("xo_all", xo_words)
         list4 = load_list("list4", offs4)
 
         w2_plane = zeroed_plane("w2_plane", R, nc.vector)
@@ -109,8 +112,9 @@ def tile_list_laggedboards_kernel(tc, xt_words, xt_scales, xo_words, xo_scales, 
         gather(xo_sc[0], xo_plane[:], list2, 0, half)
         w2_sc = deal("w2_sc", w2_plane, U8, 16)
         w_raw = load_words("w_raw", w_words, "w2_plane")
+        w2_codes = deal("w2_codes", w2_raw, I32, 4)
+        w0_raw = load_words("w0_raw", w0_words, "w2_raw")
         gather(xo_codes[0], xo_window, list2, 0, half)
-        w2_codes = deal("w2_codes_first", w2_raw, I32, 4, 0, 1)
 
         def b_piece(t, halves, bank):
             acc = ps.tile([P, len(halves), half], F32, name="acc_b%d_%d" % (t, halves[0]), tag="bank%d" % bank)
@@ -131,8 +135,6 @@ def tile_list_laggedboards_kernel(tc, xt_words, xt_scales, xo_words, xo_scales, 
         xo_codes.append(tile("xo_codes1", [P, half], U32))
         gather(xo_sc[1], xo_plane[:], list2, half, J)
         gather(xo_codes[1], xo_window, list2, half, J)
-        w2_codes.extend(deal("w2_codes_rest", w2_raw, I32, 4, 1, PACK))
-        w0_raw = load_words("w0_raw", w0_words, "w2_raw")
         b_piece(0, (1,), 1)
         for t in range(1, PACK):
             if t > 1:
@@ -186,7 +188,6 @@ def tile_list_laggedboards_kernel(tc, xt_words, xt_scales, xo_words, xo_scales, 
             difference(d23[k][:, 0, :], 2, k * CHUNK, (k + 1) * CHUNK)
         for k in (3, 2, 1, 0):
             difference(d23[k][:, 1, :], 3, k * CHUNK, (k + 1) * CHUNK)
-        out_v = out.rearrange("(h p) c -> p h c", p=P)
         for k in (3, 2, 1):
             nc.scalar.activation(hid[k][:, :, 2:4], d23[k][:].rearrange("p t c -> p c t"), ACT.Abs)
         pair = d23[0][:].rearrange("p t c -> p c t")
@@ -197,15 +198,24 @@ def tile_list_laggedboards_kernel(tc, xt_words, xt_scales, xo_words, xo_scales, 
             hq = tile("hq%d" % k, [P, CHUNK], U32)
             hs = tile("hs%d" % k, [P, CHUNK], U8)
             nc.vector.quantize_mx(out=hq[:].bitcast(E4M3), scales=hs[:], in_=hid[k][:].rearrange("p c t -> p (c t)"))
-            acc = ps.tile([P, N // P, CHUNK], F32, name="acc_o%d" % k, tag="bank%d" % (1 + k))
+            if k != order[-1]:
+                acc = ps.tile([P, N // P, CHUNK], F32, name="acc_o%d" % k, tag="bank%d" % (1 + k))
+                parts = [acc[:, h, :] for h in range(N // P)]
+                sums.append(acc)
+            else:
+                parts = [ps.tile([P, CHUNK], F32, name="acc_last%d" % h, tag="bank%d" % (2 + 3 * h))[:] for h in range(N // P)]
+                sums.append(parts)
             for h in range(N // P):
                 cols = slice(h * P, (h + 1) * P)
-                nc.tensor.matmul_mx(out=acc[:, h, :], lhsT=wb_codes[:, cols].bitcast(E4M3), lhsT_scale=wb_plane[:, cols],
+                nc.tensor.matmul_mx(out=parts[h], lhsT=wb_codes[:, cols].bitcast(E4M3), lhsT_scale=wb_plane[:, cols],
                                     rhs=hq[:].bitcast(E4M3), rhs_scale=hs[:], start=True, stop=True)
-            sums.append(acc)
+        out_v = out.rearrange("(h p) c -> p h c", p=P)
         for k, acc in zip(order, sums):
             res = tile("res%d" % k, [P, N // P, CHUNK], F32)
-            if k == 0:
+            if k == order[-1]:
+                nc.vector.tensor_copy(res[:, 0, :], acc[0])
+                nc.scalar.copy(res[:, 1, :], acc[1])
+            elif k == 0:
                 nc.vector.tensor_copy(res[:], acc[:])
             else:
                 nc.scalar.copy(res[:], acc[:])

from contextlib import ExitStack

import concourse.mybir as mybir

K, T, J, R, F, Z, C, N = 512, 1024, 256, 512, 512, 1024, 512, 256
FLOPS = 2 * K * R * J + 2 * 2 * F * R * J + 2 * R * N * C

F32 = mybir.dt.float32
BF16 = mybir.dt.bfloat16
I32 = mybir.dt.int32
U32 = mybir.dt.uint32
U16 = mybir.dt.uint16
U8 = mybir.dt.uint8
E4M3 = mybir.dt.float8_e4m3fn_x4
E5M2 = mybir.dt.float8_e5m2_x4
E2M1 = mybir.dt.float4_e2m1fn_x4
ACT = mybir.ActivationFunctionType
ALU = mybir.AluOpType

P = 128
PACK = 4
QUADS = 4
CHUNK = 128
CHUNKS = C // CHUNK


def tile_list_laggedboards_kernel(tc, xt_words, xt_scales, xo_words, xo_scales, w_words, w_scales,
                                        w0_words, w0_scales, w2_words, w2_scales, wb_words, wb_scales,
                                        offs, offs2, offs3, offs4, out):
    nc = tc.nc
    with ExitStack() as ctx:
        sb = ctx.enter_context(tc.tile_pool(name="sb", bufs=1))
        ps = ctx.enter_context(tc.psum_pool(name="ps", bufs=1))

        def tile(name, shape, dtype, tag=None):
            return sb.tile(shape, dtype, name=name, tag=tag or name, align_bytes=64)

        def load_list(name, src):
            lst = sb.tile([P, J // 16], U16, name=name)
            nc.sync.dma_start(lst[:], src)
            return lst

        def load_words(name, src, tag=None):
            words = tile(name, [P, src.shape[2]], I32, tag)
            nc.sync.dma_start(words[:], src[0].rearrange("p n t -> p (n t)").bitcast(I32))
            return words

        def zeroed_plane(name, width, engine):
            plane = tile(name, [P, width], U8)
            engine.memset(plane[:].bitcast(I32), 0)
            return plane

        def load_plane(plane, src):
            for q in range(QUADS):
                nc.sync.dma_start(plane[32 * q:32 * q + 4, :].bitcast(I32), src[0, 4 * q:4 * q + 4, :].bitcast(I32))

        def stage_rows(stage, slot, src):
            nc.sync.dma_start(stage[:, :, slot, :], src[0].bitcast(I32).rearrange("(q r) n -> r q n", r=4))

        def spread_rows(plane, stage):
            for q in range(QUADS):
                nc.vector.tensor_copy(plane[32 * q:32 * q + 4, :].bitcast(I32),
                                      stage[:, q, :, :].rearrange("r s n -> r (s n)"))

        def deal(name, raw, dtype, run, t0=0, t1=PACK):
            dealt = tile(name, [P, t1 - t0, P], dtype)
            src = raw[:].rearrange("p (b i t) -> p b t i", i=run, t=PACK)[:, :, t0:t1, :]
            nc.vector.tensor_copy(dealt[:].rearrange("p t (b i) -> p b t i", i=run), src)
            return [dealt[:, t, :] for t in range(t1 - t0)]

        def gather(picked, window, lst, lo, hi):
            nc.vector.tensor_copy(picked[:], window.indirect(lst[:, lo // 16:hi // 16]))

        def board(name, engine, tag=None):
            page = tile(name, [P, C], F32, tag)
            engine.memset(page[:].bitcast(I32), 0)
            return page

        xo_plane = tile("xo_plane", [P, Z], U8)
        list2 = load_list("list2", offs2)
        w2_stage = tile("w2_stage", [4, QUADS, 1, R // 4], I32)
        stage_rows(w2_stage, 0, w2_scales)
        for q in range(QUADS):
            rows = xo_scales[0, 4 * q:4 * q + 4, :].bitcast(I32)
            nc.sync.dma_start(xo_plane[32 * q:32 * q + 32, :].bitcast(I32),
                              rows.unsqueeze(0).broadcast_to([8, 4, Z // 4]))
        w2_raw = load_words("w2_raw", w2_words)
        xo_all = load_words("xo_all", xo_words)
        list4 = load_list("list4", offs4)

        w2_plane = zeroed_plane("w2_plane", R, nc.vector)
        pb = [board("pb0", nc.vector)]

        list1 = load_list("list1", offs)
        list3 = load_list("list3", offs3)
        xt_plane = zeroed_plane("xt_plane", T, nc.gpsimd)
        load_plane(xt_plane[:], xt_scales)
        w_plane = zeroed_plane("w_plane", R, nc.gpsimd)
        load_plane(w_plane[:], w_scales)
        w0_plane = zeroed_plane("w0_plane", R, nc.gpsimd)
        load_plane(w0_plane[:], w0_scales)
        wb_plane = zeroed_plane("wb_plane", N, nc.gpsimd)
        pb.append(board("pb1", nc.gpsimd))

        half = J // 2
        xo_window = xo_all[:].bitcast(U32)
        spread_rows(w2_plane, w2_stage)
        xt_all = tile("xt_all", [P, T], U16, "w2_stage")
        nc.sync.dma_start(xt_all[:].bitcast(I32), xt_words[0].bitcast(I32))
        xo_sc = [tile("xo_sc0", [P, half], U8)]
        xo_codes = [tile("xo_codes0", [P, half], U32)]
        gather(xo_sc[0], xo_plane[:], list2, 0, half)
        w2_sc = deal("w2_sc", w2_plane, U8, 16)
        w_raw = load_words("w_raw", w_words, "w2_plane")
        w2_codes = deal("w2_codes", w2_raw, I32, 4)
        w0_raw = load_words("w0_raw", w0_words, "w2_raw")
        gather(xo_codes[0], xo_window, list2, 0, half)

        def b_piece(t, halves, bank):
            acc = ps.tile([P, len(halves), half], F32, name="acc_b%d_%d" % (t, halves[0]), tag="bank%d" % bank)
            for i, u in enumerate(halves):
                nc.tensor.matmul_mx(out=acc[:, i, :], lhsT=w2_codes[t].bitcast(E4M3), lhsT_scale=w2_sc[t],
                                    rhs=xo_codes[u][:].bitcast(E5M2), rhs_scale=xo_sc[u][:], start=True, stop=True)
            vals = tile("b%d_%d" % (t, halves[0]), [P, len(halves) * half], F32)
            flat = acc[:].rearrange("p u j -> p (u j)")
            if bank == 0:
                nc.scalar.activation(vals[:], flat, ACT.Copy)
            else:
                nc.vector.tensor_copy(vals[:], flat)
            lo, hi = halves[0] * half, (halves[-1] + 1) * half
            nc.scalar.activation(pb[t][:].indirect(list4[:, lo // 16:hi // 16]), vals[:], ACT.Copy)

        b_piece(0, (0,), 0)
        xo_sc.append(tile("xo_sc1", [P, half], U8))
        xo_codes.append(tile("xo_codes1", [P, half], U32))
        gather(xo_sc[1], xo_plane[:], list2, half, J)
        gather(xo_codes[1], xo_window, list2, half, J)
        b_piece(0, (1,), 1)
        for t in range(1, PACK):
            if t > 1:
                pb.append(board("pb%d" % t, nc.gpsimd, ("xo_all", "xo_plane")[t - 2]))
            b_piece(t, (0, 1), 1 + t)

        xt_sc = tile("xt_sc", [P, J], U8)
        xt_codes = tile("xt_codes", [P, J], U16)
        gather(xt_codes, xt_all[:], list1, 0, J)
        w_codes = deal("w_codes", w_raw, I32, 4)
        w0_codes = deal("w0_codes", w0_raw, I32, 4)
        gather(xt_sc, xt_plane[:], list1, 0, J)
        w_sc = deal("w_sc", w_plane, U8, 16)
        w0_sc = deal("w0_sc", w0_plane, U8, 16)

        wb_codes = load_words("wb_codes", wb_words, "w_plane")
        load_plane(wb_plane[:], wb_scales)

        pa = []
        for t in range(PACK):
            acc = ps.tile([P, J], F32, name="acc_a%d" % t, tag="bank%d" % ((5 + t) % 8))
            nc.tensor.matmul_mx(out=acc[:], lhsT=w_codes[t].bitcast(E5M2), lhsT_scale=w_sc[t],
                                rhs=xt_codes[:].bitcast(E2M1), rhs_scale=xt_sc[:], start=True, stop=False)
            for u in range(2):
                nc.tensor.matmul_mx(out=acc[:, u * half:(u + 1) * half], lhsT=w0_codes[t].bitcast(E4M3),
                                    lhsT_scale=w0_sc[t], rhs=xo_codes[u][:].bitcast(E5M2),
                                    rhs_scale=xo_sc[u][:], start=False, stop=(u == 1))
            vals = tile("a%d" % t, [P, J], F32)
            nc.vector.tensor_copy(vals[:], acc[:])
            page = board("pa%d" % t, nc.gpsimd, ("w2_stage", "w2_plane", "xt_plane", "w2_raw")[t])
            nc.scalar.activation(page[:].indirect(list3[:]), vals[:], ACT.Copy)
            pa.append(page)

        def difference(dst, t, lo, hi):
            first = max(lo, 1)
            nc.vector.tensor_tensor(dst[:, first - lo:hi - lo], pa[t][:, first:hi], pb[t][:, first - 1:hi - 1],
                                    ALU.subtract)
            if lo == 0:
                nc.vector.tensor_copy(dst[:, 0:1], pa[t][:, 0:1])

        mag01 = tile("mag01", [P, 2, C], F32)
        for t in range(2):
            diff = tile("diff%d" % t, [P, C], F32)
            difference(diff, t, 0, C)
            nc.vector.scalar_tensor_tensor(mag01[:, t, :], diff[:], -1.0, diff[:], ALU.mult, ALU.max)
        hid = [tile("hid%d" % k, [P, CHUNK, PACK], BF16) for k in range(CHUNKS)]
        for k in range(CHUNKS):
            nc.vector.tensor_copy(hid[k][:, :, 0:2], mag01[:, :, k * CHUNK:(k + 1) * CHUNK].rearrange("p t c -> p c t"))
        d23 = [tile("d23_%d" % k, [P, 2, CHUNK], F32) for k in range(CHUNKS)]
        for k in range(CHUNKS):
            difference(d23[k][:, 0, :], 2, k * CHUNK, (k + 1) * CHUNK)
        for k in (3, 2, 1, 0):
            difference(d23[k][:, 1, :], 3, k * CHUNK, (k + 1) * CHUNK)
        for k in (3, 2, 1):
            nc.scalar.activation(hid[k][:, :, 2:4], d23[k][:].rearrange("p t c -> p c t"), ACT.Abs)
        pair = d23[0][:].rearrange("p t c -> p c t")
        nc.vector.scalar_tensor_tensor(hid[0][:, :, 2:4], pair, -1.0, pair, ALU.mult, ALU.max)
        order = (3, 2, 0, 1)
        sums = []
        for k in order:
            hq = tile("hq%d" % k, [P, CHUNK], U32)
            hs = tile("hs%d" % k, [P, CHUNK], U8)
            nc.vector.quantize_mx(out=hq[:].bitcast(E4M3), scales=hs[:], in_=hid[k][:].rearrange("p c t -> p (c t)"))
            if k != order[-1]:
                acc = ps.tile([P, N // P, CHUNK], F32, name="acc_o%d" % k, tag="bank%d" % (1 + k))
                parts = [acc[:, h, :] for h in range(N // P)]
                sums.append(acc)
            else:
                parts = [ps.tile([P, CHUNK], F32, name="acc_last%d" % h, tag="bank%d" % (2 + 3 * h))[:] for h in range(N // P)]
                sums.append(parts)
            for h in range(N // P):
                cols = slice(h * P, (h + 1) * P)
                nc.tensor.matmul_mx(out=parts[h], lhsT=wb_codes[:, cols].bitcast(E4M3), lhsT_scale=wb_plane[:, cols],
                                    rhs=hq[:].bitcast(E4M3), rhs_scale=hs[:], start=True, stop=True)
        out_v = out.rearrange("(h p) c -> p h c", p=P)
        for k, acc in zip(order, sums):
            res = tile("res%d" % k, [P, N // P, CHUNK], F32)
            if k == order[-1]:
                nc.vector.tensor_copy(res[:, 0, :], acc[0])
                nc.scalar.copy(res[:, 1, :], acc[1])
            elif k == 0:
                nc.vector.tensor_copy(res[:], acc[:])
            else:
                nc.scalar.copy(res[:], acc[:])
            nc.sync.dma_start(out_v[:, :, k * CHUNK:(k + 1) * CHUNK], res[:])
